import numpy as np
import ml_dtypes


def mxq(x, axis, fmt="e4m3"):
    dtype, down = {"e4m3": (ml_dtypes.float8_e4m3fn, 7), "e5m2": (ml_dtypes.float8_e5m2, 14)}[fmt]
    v = np.moveaxis(np.asarray(x, np.float32).astype(ml_dtypes.bfloat16).astype(np.float64), axis, -1)
    blocks = v.reshape(v.shape[:-1] + (-1, 32))
    amax = np.abs(blocks).max(-1, keepdims=True)
    byte = np.maximum(np.where(amax > 0, np.frexp(amax)[1] - 1 + 127, 0) - down, 1)
    scale = np.exp2(byte - 127.0)
    codes = (blocks / scale).astype(np.float32).astype(dtype).astype(np.float64)
    return np.moveaxis((codes * scale).reshape(v.shape), -1, axis)


WIDE = False


def mx_kscale(k):
    if not WIDE:
        return np.ones(k)
    levels = np.array([10, -10, 5, -5, 0])
    if k % 512:
        return np.exp2(np.random.permutation(np.resize(levels, k // 32))).repeat(32)
    a = np.empty((k // 512, 16))
    for p in range(k // 512):
        a[p, :8] = np.random.permutation(np.resize(levels, 8))
        for g in range(8):
            far = levels[np.abs(levels - a[p, g]) >= 10]
            a[p, g + 8] = far[np.random.randint(len(far))]
    return np.exp2(a.ravel()).repeat(32)


def f64(x):
    return np.asarray(x).astype(np.float64)


def striped(idx):
    return np.tile(idx.reshape(-1, 16).T, (8, 1)).astype(np.uint16)


def unstriped(offs):
    return offs[:16].T.reshape(-1).astype(np.int64)


K, T, E, C, N = 512, 1024, 4, 128, 256


def by_expert(wq, xq):
    return np.concatenate([wq[e].T @ xq[:, e * C:(e + 1) * C] for e in range(E)], axis=1)


def setup_inputs():
    n = np.random.standard_normal
    s = mx_kscale(K)[:, None]
    return {
        "xT": (n((K, T)) * s).astype(np.float32),
        "w": (n((E, K, N)) / np.sqrt(K) / s[None]).astype(np.float32),
        "gate": np.tile(np.random.uniform(0.2, 1.0, E * C), (N, 1)).astype(np.float32),
        "offs": striped(np.random.permutation(T)[:E * C]),
    }


def reference(xT, w, gate, offs):
    idx = unstriped(offs)
    xq = mxq(f64(xT)[:, idx], 0, "e4m3")
    y = by_expert(mxq(f64(w), 1, "e4m3"), xq)
    out = np.zeros((N, T))
    out[:, idx] = f64(gate) * y
    return out

@@ -1,0 +1,154 @@
+from contextlib import ExitStack
+
+import concourse.mybir as mybir
+
+K, T, E, C, N = 512, 1024, 4, 128, 256
+FLOPS = 2 * K * N * E * C
+
+F32 = mybir.dt.float32
+BF16 = mybir.dt.bfloat16
+U32 = mybir.dt.uint32
+U16 = mybir.dt.uint16
+U8 = mybir.dt.uint8
+FP8X4 = mybir.dt.float8_e4m3fn_x4
+MULT = mybir.AluOpType.mult
+ADD = mybir.AluOpType.add
+
+P = 128
+PACK = 4
+S = E * C
+NB = N // P
+
+SCATTER = "d"
+XI = ["v","v","v","v"]
+WI = [["s","s"],["s","s"],["s","s"],["s","s"]]
+DMA_ORDER = ["x0","x1","x2","x3","w0","g0","g1","w1","w2","w3"]
+
+
+def tile_routed_moe_kernel(tc, xT, w, gate, offs, out):
+    nc = tc.nc
+    with ExitStack() as ctx:
+        lists = ctx.enter_context(tc.tile_pool(name="lists", bufs=1))
+        keep = ctx.enter_context(tc.tile_pool(name="keep", bufs=1))
+        psum = ctx.enter_context(tc.psum_pool(name="psum", bufs=1))
+
+        offsets = lists.tile([P, S // 16], U16, name="offsets")
+        nc.sync.dma_start(offsets[:], offs)
+
+        def offs_of(s0, n):
+            return offsets[:, s0 // 16 : (s0 + n) // 16]
+
+        x_view = xT.rearrange("(p t) n -> p t n", t=PACK)
+        planes = [keep.tile([P, T], F32, name="plane%d" % t) for t in range(PACK)]
+        w_raw = [keep.tile([P, PACK, N], F32, name="w_raw%d" % e) for e in range(E)]
+        gate_sb = keep.tile([P, NB, S], F32, name="gate_sb")
+        for item in DMA_ORDER:
+            kind, i = item[0], int(item[1])
+            if kind == "x":
+                nc.sync.dma_start(planes[i][:], x_view[:, i, :])
+            elif kind == "w":
+                nc.sync.dma_start(w_raw[i][:], w[i].rearrange("(p j) n -> p j n", j=PACK))
+            else:
+                nc.sync.dma_start(gate_sb[:, i, :], gate[i * P : (i + 1) * P, :])
+
+        warm = keep.tile([P, 1], F32, name="warm")
+        warm_out = keep.tile([P, 1], F32, name="warm_out")
+        nc.vector.memset(warm[:], 0.0)
+        nc.scalar.copy(warm_out[:], warm[:])
+
+        windows = []
+        for b in range(NB):
+            window = keep.tile([P, T], F32, name="window%d" % b)
+            nc.vector.memset(window[:], 0.0)
+            windows.append(window)
+
+        g4 = keep.tile([P, PACK, S], F32, name="g4")
+        xg = keep.tile([P, S, PACK], BF16, name="xg", align_bytes=64)
+        x_codes = keep.tile([P, S], U32, name="x_codes", align_bytes=64)
+        x_scales = keep.tile([P, S], U8, name="x_scales", align_bytes=64)
+        wg = [keep.tile([P, N, PACK], BF16, name="wg%d" % e, align_bytes=64) for e in range(E)]
+        w_codes = [keep.tile([P, N], U32, name="w_codes%d" % e, align_bytes=64) for e in range(E)]
+        w_scales = [keep.tile([P, N], U8, name="w_scales%d" % e, align_bytes=64) for e in range(E)]
+
+        def cast(engine, dst, src):
+            if engine == "v":
+                nc.vector.tensor_copy(out=dst, in_=src)
+            elif engine == "s":
+                nc.scalar.copy(out=dst, in_=src)
+            else:
+                nc.gpsimd.tensor_scalar(dst, src, 1.0, 0.0, MULT, ADD)
+
+        def gather(t, s0, n):
+            nc.vector.tensor_copy(g4[:, t, s0 : s0 + n], planes[t][:].indirect(offs_of(s0, n)))
+
+        def x_interleave(engine, s0, n):
+            cast(engine, xg[:, s0 : s0 + n, :], g4[:, :, s0 : s0 + n].rearrange("p t c -> p c t"))
+
+        def x_quantize(s0, n):
+            nc.vector.quantize_mx(
+                out=x_codes[:, s0 : s0 + n].bitcast(FP8X4),
+                scales=x_scales[:, s0 : s0 + n],
+                in_=xg[:, s0 : s0 + n, :].rearrange("p c t -> p (c t)"),
+            )
+
+        def w_interleave(engine, e, n0, n):
+            cast(engine, wg[e][:, n0 : n0 + n, :], w_raw[e][:, :, n0 : n0 + n].rearrange("p j n -> p n j"))
+
+        def w_quantize(e, n0, n):
+            nc.vector.quantize_mx(
+                out=w_codes[e][:, n0 : n0 + n].bitcast(FP8X4),
+                scales=w_scales[e][:, n0 : n0 + n],
+                in_=wg[e][:, n0 : n0 + n, :].rearrange("p n j -> p (n j)"),
+            )
+
+        def w_prepare(e):
+            if WI[e][0] == WI[e][1] and e not in []:
+                w_interleave(WI[e][0], e, 0, N)
+                w_quantize(e, 0, N)
+            else:
+                for b in range(NB):
+                    w_interleave(WI[e][b], e, b * P, P)
+                for b in range(NB):
+                    w_quantize(e, b * P, P)
+
+        def expert(e):
+            acc = psum.tile([P, NB, C], F32, name="acc%d" % e)
+            for b in range(NB):
+                nc.tensor.matmul_mx(
+                    out=acc[:, b, :],
+                    lhsT=w_codes[e][:, b * P : (b + 1) * P].bitcast(FP8X4),
+                    lhsT_scale=w_scales[e][:, b * P : (b + 1) * P],
+                    rhs=x_codes[:, e * C : (e + 1) * C].bitcast(FP8X4),
+                    rhs_scale=x_scales[:, e * C : (e + 1) * C],
+                    start=True,
+                    stop=True,
+                )
+            y_sb = keep.tile([P, NB, C], F32, name="y%d" % e)
+            if SCATTER == "d":
+                nc.scalar.copy(out=y_sb[:], in_=acc[:])
+                for b in range(NB):
+                    nc.vector.tensor_tensor(
+                        windows[b][:].indirect(offs_of(e * C, C)), y_sb[:, b, :], gate_sb[:, b, e * C : (e + 1) * C], MULT
+                    )
+            else:
+                nc.vector.tensor_tensor(y_sb[:], acc[:], gate_sb[:, :, e * C : (e + 1) * C], MULT)
+                for b in range(NB):
+                    nc.vector.tensor_copy(windows[b][:].indirect(offs_of(e * C, C)), y_sb[:, b, :])
+
+        for t in range(PACK - 1):
+            gather(t, 0, 256)
+            gather(t, 256, 256)
+        gather(3, 0, 256)
+        x_interleave(XI[0], 0, 256)
+        gather(3, 256, 256)
+        x_quantize(0, 256)
+        x_interleave(XI[2], 256, 256)
+        w_prepare(0)
+        x_quantize(256, 256)
+        expert(0)
+        for e in range(1, E):
+            w_prepare(e)
+            expert(e)
+
+        for b in range(NB):
+            nc.sync.dma_start(out[b * P : (b + 1) * P, :], windows[b][:])

@@ -19,7 +19,7 @@ PACK = 4
 S = E * C
 NB = N // P
 
-SCATTER = "d"
+SCATTER = "e"
 XI = ["v","v","v","v"]
 WI = [["s","s"],["s","s"],["s","s"],["s","s"]]
 DMA_ORDER = ["x0","x1","x2","x3","w0","g0","g1","w1","w2","w3"]

@@ -19,10 +19,7 @@ PACK = 4
 S = E * C
 NB = N // P
 
-SCATTER = "e"
-XI = ["v","v","v","v"]
-WI = [["s","s"],["s","s"],["s","s"],["s","s"]]
-DMA_ORDER = ["x0","x1","x2","x3","w0","g0","g1","w1","w2","w3"]
+DMA_ORDER = ["x0","x1","x2","x3","w0","w1","g0","g1","w2","w3"]
 
 
 def tile_routed_moe_kernel(tc, xT, w, gate, offs, out):
@@ -39,13 +36,13 @@ def tile_routed_moe_kernel(tc, xT, w, gate, offs, out):
             return offsets[:, s0 // 16 : (s0 + n) // 16]
 
         x_view = xT.rearrange("(p t) n -> p t n", t=PACK)
-        planes = [keep.tile([P, T], F32, name="plane%d" % t) for t in range(PACK)]
+        planes = [keep.tile([P, 2 * T], F32, name="plane%d" % t) for t in range(PACK)]
         w_raw = [keep.tile([P, PACK, N], F32, name="w_raw%d" % e) for e in range(E)]
         gate_sb = keep.tile([P, NB, S], F32, name="gate_sb")
         for item in DMA_ORDER:
             kind, i = item[0], int(item[1])
             if kind == "x":
-                nc.sync.dma_start(planes[i][:], x_view[:, i, :])
+                nc.sync.dma_start(planes[i][:, 0:T], x_view[:, i, :])
             elif kind == "w":
                 nc.sync.dma_start(w_raw[i][:], w[i].rearrange("(p j) n -> p j n", j=PACK))
             else:
@@ -66,9 +63,11 @@ def tile_routed_moe_kernel(tc, xT, w, gate, offs, out):
         xg = keep.tile([P, S, PACK], BF16, name="xg", align_bytes=64)
         x_codes = keep.tile([P, S], U32, name="x_codes", align_bytes=64)
         x_scales = keep.tile([P, S], U8, name="x_scales", align_bytes=64)
-        wg = [keep.tile([P, N, PACK], BF16, name="wg%d" % e, align_bytes=64) for e in range(E)]
-        w_codes = [keep.tile([P, N], U32, name="w_codes%d" % e, align_bytes=64) for e in range(E)]
-        w_scales = [keep.tile([P, N], U8, name="w_scales%d" % e, align_bytes=64) for e in range(E)]
+        wg = keep.tile([P, E * N, PACK], BF16, name="wg", align_bytes=64)
+        w_codes = keep.tile([P, E * N], U32, name="w_codes", align_bytes=64)
+        w_scales = keep.tile([P, E * N], U8, name="w_scales", align_bytes=64)
+        acc = [psum.tile([P, NB, C], F32, name="acc%d" % e) for e in range(E)]
+        y_sb = keep.tile([P, NB, S], F32, name="y_sb")
 
         def cast(engine, dst, src):
             if engine == "v":
@@ -78,77 +77,83 @@ def tile_routed_moe_kernel(tc, xT, w, gate, offs, out):
             else:
                 nc.gpsimd.tensor_scalar(dst, src, 1.0, 0.0, MULT, ADD)
 
-        def gather(t, s0, n):
+        def g(t, s0, n):
             nc.vector.tensor_copy(g4[:, t, s0 : s0 + n], planes[t][:].indirect(offs_of(s0, n)))
 
-        def x_interleave(engine, s0, n):
+        def xi(engine, s0, n):
             cast(engine, xg[:, s0 : s0 + n, :], g4[:, :, s0 : s0 + n].rearrange("p t c -> p c t"))
 
-        def x_quantize(s0, n):
+        def xp(engine, u, s0, n):
+            cast(
+                engine,
+                xg[:, s0 : s0 + n, 2 * u : 2 * u + 2],
+                g4[:, 2 * u : 2 * u + 2, s0 : s0 + n].rearrange("p t c -> p c t"),
+            )
+
+        def xq(s0, n):
             nc.vector.quantize_mx(
                 out=x_codes[:, s0 : s0 + n].bitcast(FP8X4),
                 scales=x_scales[:, s0 : s0 + n],
                 in_=xg[:, s0 : s0 + n, :].rearrange("p c t -> p (c t)"),
             )
 
-        def w_interleave(engine, e, n0, n):
-            cast(engine, wg[e][:, n0 : n0 + n, :], w_raw[e][:, :, n0 : n0 + n].rearrange("p j n -> p n j"))
+        def wi(engine, e, n0=0, n=N):
+            cast(engine, wg[:, e * N + n0 : e * N + n0 + n, :], w_raw[e][:, :, n0 : n0 + n].rearrange("p j n -> p n j"))
 
-        def w_quantize(e, n0, n):
+        def wq(c0, n):
             nc.vector.quantize_mx(
-                out=w_codes[e][:, n0 : n0 + n].bitcast(FP8X4),
-                scales=w_scales[e][:, n0 : n0 + n],
-                in_=wg[e][:, n0 : n0 + n, :].rearrange("p n j -> p (n j)"),
+                out=w_codes[:, c0 : c0 + n].bitcast(FP8X4),
+                scales=w_scales[:, c0 : c0 + n],
+                in_=wg[:, c0 : c0 + n, :].rearrange("p n j -> p (n j)"),
             )
 
-        def w_prepare(e):
-            if WI[e][0] == WI[e][1] and e not in []:
-                w_interleave(WI[e][0], e, 0, N)
-                w_quantize(e, 0, N)
-            else:
-                for b in range(NB):
-                    w_interleave(WI[e][b], e, b * P, P)
-                for b in range(NB):
-                    w_quantize(e, b * P, P)
-
-        def expert(e):
-            acc = psum.tile([P, NB, C], F32, name="acc%d" % e)
+        def mm(e):
             for b in range(NB):
+                c0 = e * N + b * P
                 nc.tensor.matmul_mx(
-                    out=acc[:, b, :],
-                    lhsT=w_codes[e][:, b * P : (b + 1) * P].bitcast(FP8X4),
-                    lhsT_scale=w_scales[e][:, b * P : (b + 1) * P],
+                    out=acc[e][:, b, :],
+                    lhsT=w_codes[:, c0 : c0 + P].bitcast(FP8X4),
+                    lhsT_scale=w_scales[:, c0 : c0 + P],
                     rhs=x_codes[:, e * C : (e + 1) * C].bitcast(FP8X4),
                     rhs_scale=x_scales[:, e * C : (e + 1) * C],
                     start=True,
                     stop=True,
                 )
-            y_sb = keep.tile([P, NB, C], F32, name="y%d" % e)
-            if SCATTER == "d":
-                nc.scalar.copy(out=y_sb[:], in_=acc[:])
-                for b in range(NB):
-                    nc.vector.tensor_tensor(
-                        windows[b][:].indirect(offs_of(e * C, C)), y_sb[:, b, :], gate_sb[:, b, e * C : (e + 1) * C], MULT
-                    )
-            else:
-                nc.vector.tensor_tensor(y_sb[:], acc[:], gate_sb[:, :, e * C : (e + 1) * C], MULT)
-                for b in range(NB):
-                    nc.vector.tensor_copy(windows[b][:].indirect(offs_of(e * C, C)), y_sb[:, b, :])
 
-        for t in range(PACK - 1):
-            gather(t, 0, 256)
-            gather(t, 256, 256)
-        gather(3, 0, 256)
-        x_interleave(XI[0], 0, 256)
-        gather(3, 256, 256)
-        x_quantize(0, 256)
-        x_interleave(XI[2], 256, 256)
-        w_prepare(0)
-        x_quantize(256, 256)
-        expert(0)
-        for e in range(1, E):
-            w_prepare(e)
-            expert(e)
+        def cp(e):
+            nc.scalar.copy(out=y_sb[:, :, e * C : (e + 1) * C], in_=acc[e][:])
 
-        for b in range(NB):
+        def sc(b, s0, n):
+            nc.vector.tensor_tensor(
+                windows[b][:].indirect(offs_of(s0, n)), y_sb[:, b, s0 : s0 + n], gate_sb[:, b, s0 : s0 + n], MULT
+            )
+
+        def st(b):
             nc.sync.dma_start(out[b * P : (b + 1) * P, :], windows[b][:])
+
+        g(0, 0, 512); g(1, 0, 512)
+        xp("s", 0, 0, 512)
+        g(2, 0, 512)
+        g(3, 0, 256)
+        xp("v", 1, 0, 256)
+        g(3, 256, 256)
+        wi("s", 0)
+        xq(0, 256)
+        wq(0, 256)
+        mm(0); cp(0)
+        xp("v", 1, 256, 256)
+        wi("s", 1)
+        xq(256, 256)
+        sc(0, 0, 128)
+        wq(256, 256); mm(1); cp(1)
+        sc(1, 0, 128)
+        wi("s", 2)
+        sc(0, 128, 128)
+        wq(512, 256); mm(2); cp(2)
+        sc(1, 128, 128)
+        wi("s", 3)
+        sc(0, 256, 128)
+        wq(768, 256); mm(3); cp(3)
+        sc(1, 256, 128)
+        sc(0, 384, 128); st(0)
+        sc(1, 384, 128); st(1)

@@ -66,7 +66,7 @@ def tile_routed_moe_kernel(tc, xT, w, gate, offs, out):
         wg = keep.tile([P, E * N, PACK], BF16, name="wg", align_bytes=64)
         w_codes = keep.tile([P, E * N], U32, name="w_codes", align_bytes=64)
         w_scales = keep.tile([P, E * N], U8, name="w_scales", align_bytes=64)
-        acc = [psum.tile([P, NB, C], F32, name="acc%d" % e) for e in range(E)]
+        acc = [[psum.tile([P, C], F32, name="acc%d_%d" % (e, b)) for b in range(NB)] for e in range(E)]
         y_sb = keep.tile([P, NB, S], F32, name="y_sb")
 
         def cast(engine, dst, src):
@@ -111,7 +111,7 @@ def tile_routed_moe_kernel(tc, xT, w, gate, offs, out):
             for b in range(NB):
                 c0 = e * N + b * P
                 nc.tensor.matmul_mx(
-                    out=acc[e][:, b, :],
+                    out=acc[e][b][:],
                     lhsT=w_codes[:, c0 : c0 + P].bitcast(FP8X4),
                     lhsT_scale=w_scales[:, c0 : c0 + P],
                     rhs=x_codes[:, e * C : (e + 1) * C].bitcast(FP8X4),
@@ -121,7 +121,8 @@ def tile_routed_moe_kernel(tc, xT, w, gate, offs, out):
                 )
 
         def cp(e):
-            nc.scalar.copy(out=y_sb[:, :, e * C : (e + 1) * C], in_=acc[e][:])
+            for b in range(NB):
+                nc.scalar.copy(out=y_sb[:, b, e * C : (e + 1) * C], in_=acc[e][b][:])
 
         def sc(b, s0, n):
             nc.vector.tensor_tensor(

@@ -13,6 +13,7 @@ U8 = mybir.dt.uint8
 FP8X4 = mybir.dt.float8_e4m3fn_x4
 MULT = mybir.AluOpType.mult
 ADD = mybir.AluOpType.add
+COPY = mybir.ActivationFunctionType.Copy
 
 P = 128
 PACK = 4
@@ -59,6 +60,7 @@ def tile_routed_moe_kernel(tc, xT, w, gate, offs, out):
             nc.vector.memset(window[:], 0.0)
             windows.append(window)
 
+        planes_bf = [keep.tile([P, T], BF16, name="plane_bf%d" % t) for t in range(2)]
         g4 = keep.tile([P, PACK, S], F32, name="g4")
         xg = keep.tile([P, S, PACK], BF16, name="xg", align_bytes=64)
         x_codes = keep.tile([P, S], U32, name="x_codes", align_bytes=64)
@@ -79,6 +81,15 @@ def tile_routed_moe_kernel(tc, xT, w, gate, offs, out):
 
         def g(t, s0, n):
             nc.vector.tensor_copy(g4[:, t, s0 : s0 + n], planes[t][:].indirect(offs_of(s0, n)))
+
+        def cb(t):
+            nc.vector.tensor_copy(out=planes_bf[t][:], in_=planes[t][:, 0:T])
+
+        def sg(t, s0, n):
+            nc.scalar.activation(xg[:, s0 : s0 + n, t], planes_bf[t][:].indirect(offs_of(s0, n)), COPY)
+
+        def gb(t, s0, n):
+            nc.vector.tensor_copy(xg[:, s0 : s0 + n, t], planes[t][:].indirect(offs_of(s0, n)))
 
         def xi(engine, s0, n):
             cast(engine, xg[:, s0 : s0 + n, :], g4[:, :, s0 : s0 + n].rearrange("p t c -> p c t"))
@@ -132,17 +143,15 @@ def tile_routed_moe_kernel(tc, xT, w, gate, offs, out):
         def st(b):
             nc.sync.dma_start(out[b * P : (b + 1) * P, :], windows[b][:])
 
-        g(0, 0, 512); g(1, 0, 512)
-        xp("s", 0, 0, 512)
-        g(2, 0, 512)
-        g(3, 0, 256)
-        xp("v", 1, 0, 256)
-        g(3, 256, 256)
+        cb(0); sg(0, 0, 512)
+        cb(1); sg(1, 0, 512)
+        gb(2, 0, 512)
+        gb(3, 0, 256)
+        gb(3, 256, 256)
         wi("s", 0)
         xq(0, 256)
         wq(0, 256)
         mm(0); cp(0)
-        xp("v", 1, 256, 256)
         wi("s", 1)
         xq(256, 256)
         sc(0, 0, 128)

@@ -109,7 +109,11 @@ def tile_routed_moe_kernel(tc, xT, w, gate, offs, out):
             )
 
         def wi(engine, e, n0=0, n=N):
-            cast(engine, wg[:, e * N + n0 : e * N + n0 + n, :], w_raw[e][:, :, n0 : n0 + n].rearrange("p j n -> p n j"))
+            cast(
+                engine,
+                wg[:, e * N + n0 : e * N + n0 + n, :].rearrange("p (c i) j -> p c j i", i=4),
+                w_raw[e][:, :, n0 : n0 + n].rearrange("p j (c i) -> p c j i", i=4),
+            )
 
         def wq(c0, n):
             nc.vector.quantize_mx(

@@ -88,9 +88,6 @@ def tile_routed_moe_kernel(tc, xT, w, gate, offs, out):
         def sg(t, s0, n):
             nc.scalar.activation(xg[:, s0 : s0 + n, t], planes_bf[t][:].indirect(offs_of(s0, n)), COPY)
 
-        def gb(t, s0, n):
-            nc.vector.tensor_copy(xg[:, s0 : s0 + n, t], planes[t][:].indirect(offs_of(s0, n)))
-
         def xi(engine, s0, n):
             cast(engine, xg[:, s0 : s0 + n, :], g4[:, :, s0 : s0 + n].rearrange("p t c -> p c t"))
 
@@ -149,13 +146,15 @@ def tile_routed_moe_kernel(tc, xT, w, gate, offs, out):
 
         cb(0); sg(0, 0, 512)
         cb(1); sg(1, 0, 512)
-        gb(2, 0, 512)
-        gb(3, 0, 256)
-        gb(3, 256, 256)
+        g(2, 0, 512)
+        g(3, 0, 256)
+        xp("v", 1, 0, 256)
+        g(3, 256, 256)
         wi("s", 0)
         xq(0, 256)
         wq(0, 256)
         mm(0); cp(0)
+        xp("v", 1, 256, 256)
         wi("s", 1)
         xq(256, 256)
         sc(0, 0, 128)

@@ -20,7 +20,7 @@ PACK = 4
 S = E * C
 NB = N // P
 
-DMA_ORDER = ["x0","x1","x2","x3","w0","w1","g0","g1","w2","w3"]
+DMA_ORDER = ["x0","o0","x1","x2","x3","w0","w1","g0","g1","w2","w3"]
 
 
 def tile_routed_moe_kernel(tc, xT, w, gate, offs, out):
@@ -31,7 +31,6 @@ def tile_routed_moe_kernel(tc, xT, w, gate, offs, out):
         psum = ctx.enter_context(tc.psum_pool(name="psum", bufs=1))
 
         offsets = lists.tile([P, S // 16], U16, name="offsets")
-        nc.sync.dma_start(offsets[:], offs)
 
         def offs_of(s0, n):
             return offsets[:, s0 // 16 : (s0 + n) // 16]
@@ -42,7 +41,9 @@ def tile_routed_moe_kernel(tc, xT, w, gate, offs, out):
         gate_sb = keep.tile([P, NB, S], F32, name="gate_sb")
         for item in DMA_ORDER:
             kind, i = item[0], int(item[1])
-            if kind == "x":
+            if kind == "o":
+                nc.sync.dma_start(offsets[:], offs)
+            elif kind == "x":
                 nc.sync.dma_start(planes[i][:, 0:T], x_view[:, i, :])
             elif kind == "w":
                 nc.sync.dma_start(w_raw[i][:], w[i].rearrange("(p j) n -> p j n", j=PACK))
@@ -94,8 +95,8 @@ def tile_routed_moe_kernel(tc, xT, w, gate, offs, out):
         def xp(engine, u, s0, n):
             cast(
                 engine,
-                xg[:, s0 : s0 + n, 2 * u : 2 * u + 2],
-                g4[:, 2 * u : 2 * u + 2, s0 : s0 + n].rearrange("p t c -> p c t"),
+                xg[:, s0 : s0 + n, 2 * u : 2 * u + 2].rearrange("p (c i) t -> p c t i", i=4),
+                g4[:, 2 * u : 2 * u + 2, s0 : s0 + n].rearrange("p t (c i) -> p c t i", i=4),
             )
 
         def xq(s0, n):

@@ -12,15 +12,17 @@ U16 = mybir.dt.uint16
 U8 = mybir.dt.uint8
 FP8X4 = mybir.dt.float8_e4m3fn_x4
 MULT = mybir.AluOpType.mult
-ADD = mybir.AluOpType.add
 COPY = mybir.ActivationFunctionType.Copy
 
 P = 128
 PACK = 4
 S = E * C
-NB = N // P
+BANDS = N // P
+HALF = S // 2
+RUN = 4
 
-DMA_ORDER = ["x0","o0","x1","x2","x3","w0","w1","g0","g1","w2","w3"]
+SCALAR_PLANES = (0, 1)
+VECTOR_PLANES = (2, 3)
 
 
 def tile_routed_moe_kernel(tc, xT, w, gate, offs, out):
@@ -31,24 +33,26 @@ def tile_routed_moe_kernel(tc, xT, w, gate, offs, out):
         psum = ctx.enter_context(tc.psum_pool(name="psum", bufs=1))
 
         offsets = lists.tile([P, S // 16], U16, name="offsets")
-
-        def offs_of(s0, n):
-            return offsets[:, s0 // 16 : (s0 + n) // 16]
-
-        x_view = xT.rearrange("(p t) n -> p t n", t=PACK)
-        planes = [keep.tile([P, 2 * T], F32, name="plane%d" % t) for t in range(PACK)]
+        planes = [keep.tile([P, T], F32, name="plane%d" % t) for t in range(PACK)]
         w_raw = [keep.tile([P, PACK, N], F32, name="w_raw%d" % e) for e in range(E)]
-        gate_sb = keep.tile([P, NB, S], F32, name="gate_sb")
-        for item in DMA_ORDER:
-            kind, i = item[0], int(item[1])
-            if kind == "o":
-                nc.sync.dma_start(offsets[:], offs)
-            elif kind == "x":
-                nc.sync.dma_start(planes[i][:, 0:T], x_view[:, i, :])
-            elif kind == "w":
-                nc.sync.dma_start(w_raw[i][:], w[i].rearrange("(p j) n -> p j n", j=PACK))
-            else:
-                nc.sync.dma_start(gate_sb[:, i, :], gate[i * P : (i + 1) * P, :])
+        gate_sb = keep.tile([P, BANDS, S], F32, name="gate_sb")
+
+        def load_plane(t):
+            nc.sync.dma_start(planes[t][:], xT.rearrange("(p t) n -> p t n", t=PACK)[:, t, :])
+
+        def load_weights(e):
+            nc.sync.dma_start(w_raw[e][:], w[e].rearrange("(p j) n -> p j n", j=PACK))
+
+        load_plane(0)
+        nc.sync.dma_start(offsets[:], offs)
+        for t in range(1, PACK):
+            load_plane(t)
+        load_weights(0)
+        load_weights(1)
+        for b in range(BANDS):
+            nc.sync.dma_start(gate_sb[:, b, :], gate[b * P : (b + 1) * P, :])
+        load_weights(2)
+        load_weights(3)
 
         warm = keep.tile([P, 1], F32, name="warm")
         warm_out = keep.tile([P, 1], F32, name="warm_out")
@@ -56,118 +60,103 @@ def tile_routed_moe_kernel(tc, xT, w, gate, offs, out):
         nc.scalar.copy(warm_out[:], warm[:])
 
         windows = []
-        for b in range(NB):
+        for b in range(BANDS):
             window = keep.tile([P, T], F32, name="window%d" % b)
             nc.vector.memset(window[:], 0.0)
             windows.append(window)
 
-        planes_bf = [keep.tile([P, T], BF16, name="plane_bf%d" % t) for t in range(2)]
-        g4 = keep.tile([P, PACK, S], F32, name="g4")
-        xg = keep.tile([P, S, PACK], BF16, name="xg", align_bytes=64)
+        planes_bf = [keep.tile([P, T], BF16, name="plane_bf%d" % t) for t in SCALAR_PLANES]
+        gathered = keep.tile([P, len(VECTOR_PLANES), S], F32, name="gathered")
+        x_grouped = keep.tile([P, S, PACK], BF16, name="x_grouped", align_bytes=64)
         x_codes = keep.tile([P, S], U32, name="x_codes", align_bytes=64)
         x_scales = keep.tile([P, S], U8, name="x_scales", align_bytes=64)
-        wg = keep.tile([P, E * N, PACK], BF16, name="wg", align_bytes=64)
+        w_grouped = keep.tile([P, E * N, PACK], BF16, name="w_grouped", align_bytes=64)
         w_codes = keep.tile([P, E * N], U32, name="w_codes", align_bytes=64)
         w_scales = keep.tile([P, E * N], U8, name="w_scales", align_bytes=64)
-        acc = [[psum.tile([P, C], F32, name="acc%d_%d" % (e, b)) for b in range(NB)] for e in range(E)]
-        y_sb = keep.tile([P, NB, S], F32, name="y_sb")
+        acc = [[psum.tile([P, C], F32, name="acc%d_%d" % (e, b)) for b in range(BANDS)] for e in range(E)]
+        y_sb = keep.tile([P, BANDS, S], F32, name="y_sb")
 
-        def cast(engine, dst, src):
-            if engine == "v":
-                nc.vector.tensor_copy(out=dst, in_=src)
-            elif engine == "s":
-                nc.scalar.copy(out=dst, in_=src)
-            else:
-                nc.gpsimd.tensor_scalar(dst, src, 1.0, 0.0, MULT, ADD)
+        def offsets_of(s0, n):
+            return offsets[:, s0 // 16 : (s0 + n) // 16]
 
-        def g(t, s0, n):
-            nc.vector.tensor_copy(g4[:, t, s0 : s0 + n], planes[t][:].indirect(offs_of(s0, n)))
+        def scalar_gather(t):
+            nc.vector.tensor_copy(out=planes_bf[t][:], in_=planes[t][:])
+            nc.scalar.activation(x_grouped[:, :, t], planes_bf[t][:].indirect(offsets[:]), COPY)
 
-        def cb(t):
-            nc.vector.tensor_copy(out=planes_bf[t][:], in_=planes[t][:, 0:T])
-
-        def sg(t, s0, n):
-            nc.scalar.activation(xg[:, s0 : s0 + n, t], planes_bf[t][:].indirect(offs_of(s0, n)), COPY)
-
-        def xi(engine, s0, n):
-            cast(engine, xg[:, s0 : s0 + n, :], g4[:, :, s0 : s0 + n].rearrange("p t c -> p c t"))
-
-        def xp(engine, u, s0, n):
-            cast(
-                engine,
-                xg[:, s0 : s0 + n, 2 * u : 2 * u + 2].rearrange("p (c i) t -> p c t i", i=4),
-                g4[:, 2 * u : 2 * u + 2, s0 : s0 + n].rearrange("p t (c i) -> p c t i", i=4),
+        def vector_gather(t, s0, n):
+            nc.vector.tensor_copy(
+                gathered[:, t - VECTOR_PLANES[0], s0 : s0 + n], planes[t][:].indirect(offsets_of(s0, n))
             )
 
-        def xq(s0, n):
+        def round_vector_planes(s0, n):
+            t0 = VECTOR_PLANES[0]
+            nc.vector.tensor_copy(
+                out=x_grouped[:, s0 : s0 + n, t0 : t0 + 2].rearrange("p (c i) t -> p c t i", i=RUN),
+                in_=gathered[:, :, s0 : s0 + n].rearrange("p t (c i) -> p c t i", i=RUN),
+            )
+
+        def quantize_slots(s0, n):
             nc.vector.quantize_mx(
                 out=x_codes[:, s0 : s0 + n].bitcast(FP8X4),
                 scales=x_scales[:, s0 : s0 + n],
-                in_=xg[:, s0 : s0 + n, :].rearrange("p c t -> p (c t)"),
+                in_=x_grouped[:, s0 : s0 + n, :].rearrange("p c t -> p (c t)"),
             )
 
-        def wi(engine, e, n0=0, n=N):
-            cast(
-                engine,
-                wg[:, e * N + n0 : e * N + n0 + n, :].rearrange("p (c i) j -> p c j i", i=4),
-                w_raw[e][:, :, n0 : n0 + n].rearrange("p j (c i) -> p c j i", i=4),
+        def group_weights(e):
+            nc.scalar.copy(
+                out=w_grouped[:, e * N : (e + 1) * N, :].rearrange("p (c i) j -> p c j i", i=RUN),
+                in_=w_raw[e][:].rearrange("p j (c i) -> p c j i", i=RUN),
             )
 
-        def wq(c0, n):
+        def multiply(e):
             nc.vector.quantize_mx(
-                out=w_codes[:, c0 : c0 + n].bitcast(FP8X4),
-                scales=w_scales[:, c0 : c0 + n],
-                in_=wg[:, c0 : c0 + n, :].rearrange("p n j -> p (n j)"),
+                out=w_codes[:, e * N : (e + 1) * N].bitcast(FP8X4),
+                scales=w_scales[:, e * N : (e + 1) * N],
+                in_=w_grouped[:, e * N : (e + 1) * N, :].rearrange("p n j -> p (n j)"),
             )
-
-        def mm(e):
-            for b in range(NB):
-                c0 = e * N + b * P
+            slots = slice(e * C, (e + 1) * C)
+            for b in range(BANDS):
+                features = slice(e * N + b * P, e * N + (b + 1) * P)
                 nc.tensor.matmul_mx(
                     out=acc[e][b][:],
-                    lhsT=w_codes[:, c0 : c0 + P].bitcast(FP8X4),
-                    lhsT_scale=w_scales[:, c0 : c0 + P],
-                    rhs=x_codes[:, e * C : (e + 1) * C].bitcast(FP8X4),
-                    rhs_scale=x_scales[:, e * C : (e + 1) * C],
+                    lhsT=w_codes[:, features].bitcast(FP8X4),
+                    lhsT_scale=w_scales[:, features],
+                    rhs=x_codes[:, slots].bitcast(FP8X4),
+                    rhs_scale=x_scales[:, slots],
                     start=True,
                     stop=True,
                 )
+            for b in range(BANDS):
+                nc.scalar.copy(out=y_sb[:, b, slots], in_=acc[e][b][:])
 
-        def cp(e):
-            for b in range(NB):
-                nc.scalar.copy(out=y_sb[:, b, e * C : (e + 1) * C], in_=acc[e][b][:])
-
-        def sc(b, s0, n):
+        def scatter(b, e):
+            slots = slice(e * C, (e + 1) * C)
             nc.vector.tensor_tensor(
-                windows[b][:].indirect(offs_of(s0, n)), y_sb[:, b, s0 : s0 + n], gate_sb[:, b, s0 : s0 + n], MULT
+                windows[b][:].indirect(offsets_of(e * C, C)), y_sb[:, b, slots], gate_sb[:, b, slots], MULT
             )
 
-        def st(b):
+        def store(b):
             nc.sync.dma_start(out[b * P : (b + 1) * P, :], windows[b][:])
 
-        cb(0); sg(0, 0, 512)
-        cb(1); sg(1, 0, 512)
-        g(2, 0, 512)
-        g(3, 0, 256)
-        xp("v", 1, 0, 256)
-        g(3, 256, 256)
-        wi("s", 0)
-        xq(0, 256)
-        wq(0, 256)
-        mm(0); cp(0)
-        xp("v", 1, 256, 256)
-        wi("s", 1)
-        xq(256, 256)
-        sc(0, 0, 128)
-        wq(256, 256); mm(1); cp(1)
-        sc(1, 0, 128)
-        wi("s", 2)
-        sc(0, 128, 128)
-        wq(512, 256); mm(2); cp(2)
-        sc(1, 128, 128)
-        wi("s", 3)
-        sc(0, 256, 128)
-        wq(768, 256); mm(3); cp(3)
-        sc(1, 256, 128)
-        sc(0, 384, 128); st(0)
-        sc(1, 384, 128); st(1)
+        for t in SCALAR_PLANES:
+            scalar_gather(t)
+        vector_gather(2, 0, S)
+        vector_gather(3, 0, HALF)
+        round_vector_planes(0, HALF)
+        vector_gather(3, HALF, HALF)
+        group_weights(0)
+        quantize_slots(0, HALF)
+        multiply(0)
+        round_vector_planes(HALF, HALF)
+        group_weights(1)
+        quantize_slots(HALF, HALF)
+
+        for e in range(1, E):
+            scatter(0, e - 1)
+            multiply(e)
+            scatter(1, e - 1)
+            if e + 1 < E:
+                group_weights(e + 1)
+        for b in range(BANDS):
+            scatter(b, E - 1)
+            store(b)

@@ -43,16 +43,21 @@ def tile_routed_moe_kernel(tc, xT, w, gate, offs, out):
         def load_weights(e):
             nc.sync.dma_start(w_raw[e][:], w[e].rearrange("(p j) n -> p j n", j=PACK))
 
+        def load_gate(s0):
+            nc.sync.dma_start(
+                gate_sb[:, :, s0 : s0 + HALF], gate.rearrange("(b p) s -> p b s", p=P)[:, :, s0 : s0 + HALF]
+            )
+
         load_plane(0)
         nc.sync.dma_start(offsets[:], offs)
         for t in range(1, PACK):
             load_plane(t)
         load_weights(0)
         load_weights(1)
-        for b in range(BANDS):
-            nc.sync.dma_start(gate_sb[:, b, :], gate[b * P : (b + 1) * P, :])
         load_weights(2)
+        load_gate(0)
         load_weights(3)
+        load_gate(HALF)
 
         warm = keep.tile([P, 1], F32, name="warm")
         warm_out = keep.tile([P, 1], F32, name="warm_out")

@@ -34,7 +34,7 @@ def tile_routed_moe_kernel(tc, xT, w, gate, offs, out):
 
         offsets = lists.tile([P, S // 16], U16, name="offsets")
         planes = [keep.tile([P, T], F32, name="plane%d" % t) for t in range(PACK)]
-        w_raw = [keep.tile([P, PACK, N], F32, name="w_raw%d" % e) for e in range(E)]
+        w_raw = [keep.tile([P, PACK, N], F32, name="w_raw%d" % e, align_bytes=64) for e in range(E)]
         gate_sb = keep.tile([P, BANDS, S], F32, name="gate_sb")
 
         def load_plane(t):
@@ -73,7 +73,10 @@ def tile_routed_moe_kernel(tc, xT, w, gate, offs, out):
         planes_bf = [keep.tile([P, T], BF16, name="plane_bf%d" % t) for t in SCALAR_PLANES]
         gathered = keep.tile([P, len(VECTOR_PLANES), S], F32, name="gathered")
         x_grouped = keep.tile([P, S, PACK], BF16, name="x_grouped", align_bytes=64)
-        x_codes = keep.tile([P, S], U32, name="x_codes", align_bytes=64)
+        x_codes = [
+            keep.tile([P, HALF], U32, name="x_codes0", align_bytes=64),
+            keep.tile([P, HALF], U32, name="x_codes1", tag="w_raw0", align_bytes=64),
+        ]
         x_scales = keep.tile([P, S], U8, name="x_scales", align_bytes=64)
         w_grouped = keep.tile([P, E * N, PACK], BF16, name="w_grouped", align_bytes=64)
         w_codes = keep.tile([P, E * N], U32, name="w_codes", align_bytes=64)
@@ -102,7 +105,7 @@ def tile_routed_moe_kernel(tc, xT, w, gate, offs, out):
 
         def quantize_slots(s0, n):
             nc.vector.quantize_mx(
-                out=x_codes[:, s0 : s0 + n].bitcast(FP8X4),
+                out=x_codes[s0 // HALF][:].bitcast(FP8X4),
                 scales=x_scales[:, s0 : s0 + n],
                 in_=x_grouped[:, s0 : s0 + n, :].rearrange("p c t -> p (c t)"),
             )
@@ -126,7 +129,7 @@ def tile_routed_moe_kernel(tc, xT, w, gate, offs, out):
                     out=acc[e][b][:],
                     lhsT=w_codes[:, features].bitcast(FP8X4),
                     lhsT_scale=w_scales[:, features],
-                    rhs=x_codes[:, slots].bitcast(FP8X4),
+                    rhs=x_codes[e * C // HALF][:, e * C % HALF : e * C % HALF + C].bitcast(FP8X4),
                     rhs_scale=x_scales[:, slots],
                     start=True,
                     stop=True,

@@ -79,6 +79,12 @@ def tile_routed_moe_kernel(tc, xT, w, gate, offs, out):
         ]
         x_scales = keep.tile([P, S], U8, name="x_scales", align_bytes=64)
         w_grouped = keep.tile([P, E * N, PACK], BF16, name="w_grouped", align_bytes=64)
+        w0_grouped = keep.tile([P, N, PACK], BF16, name="w0_grouped", align_bytes=64)
+        w1_band1 = keep.tile([P, P, PACK], BF16, name="w1_band1", tag="w0_grouped", align_bytes=64)
+
+        def grouped_weights(e):
+            return w0_grouped[:] if e == 0 else w_grouped[:, e * N : (e + 1) * N, :]
+
         w_codes = keep.tile([P, E * N], U32, name="w_codes", align_bytes=64)
         w_scales = keep.tile([P, E * N], U8, name="w_scales", align_bytes=64)
         acc = [[psum.tile([P, C], F32, name="acc%d_%d" % (e, b)) for b in range(BANDS)] for e in range(E)]
@@ -112,16 +118,38 @@ def tile_routed_moe_kernel(tc, xT, w, gate, offs, out):
 
         def group_weights(e):
             nc.scalar.copy(
-                out=w_grouped[:, e * N : (e + 1) * N, :].rearrange("p (c i) j -> p c j i", i=RUN),
+                out=grouped_weights(e).rearrange("p (c i) j -> p c j i", i=RUN),
                 in_=w_raw[e][:].rearrange("p j (c i) -> p c j i", i=RUN),
             )
 
-        def multiply(e):
+        def group_w1_shared():
+            nc.scalar.copy(
+                out=w_grouped[:, N : N + P, :].rearrange("p (c i) j -> p c j i", i=RUN),
+                in_=w_raw[1][:, :, :P].rearrange("p j (c i) -> p c j i", i=RUN),
+            )
+            nc.vector.tensor_copy(
+                out=w1_band1[:].rearrange("p (c i) j -> p c j i", i=RUN),
+                in_=w_raw[1][:, :, P:].rearrange("p j (c i) -> p c j i", i=RUN),
+            )
+
+        def quantize_weights(e):
+            if e == 1:
+                for b, grouped in enumerate((w_grouped[:, N : N + P, :], w1_band1[:])):
+                    features = slice(N + b * P, N + (b + 1) * P)
+                    nc.vector.quantize_mx(
+                        out=w_codes[:, features].bitcast(FP8X4),
+                        scales=w_scales[:, features],
+                        in_=grouped.rearrange("p n j -> p (n j)"),
+                    )
+                return
             nc.vector.quantize_mx(
                 out=w_codes[:, e * N : (e + 1) * N].bitcast(FP8X4),
                 scales=w_scales[:, e * N : (e + 1) * N],
-                in_=w_grouped[:, e * N : (e + 1) * N, :].rearrange("p n j -> p (n j)"),
+                in_=grouped_weights(e).rearrange("p n j -> p (n j)"),
             )
+
+        def multiply(e):
+            quantize_weights(e)
             slots = slice(e * C, (e + 1) * C)
             for b in range(BANDS):
                 features = slice(e * N + b * P, e * N + (b + 1) * P)
@@ -156,8 +184,8 @@ def tile_routed_moe_kernel(tc, xT, w, gate, offs, out):
         quantize_slots(0, HALF)
         multiply(0)
         round_vector_planes(HALF, HALF)
-        group_weights(1)
         quantize_slots(HALF, HALF)
+        group_w1_shared()
 
         for e in range(1, E):
             scatter(0, e - 1)

from contextlib import ExitStack

import concourse.mybir as mybir

K, T, E, C, N = 512, 1024, 4, 128, 256
FLOPS = 2 * K * N * E * C

F32 = mybir.dt.float32
BF16 = mybir.dt.bfloat16
U32 = mybir.dt.uint32
U16 = mybir.dt.uint16
U8 = mybir.dt.uint8
FP8X4 = mybir.dt.float8_e4m3fn_x4
MULT = mybir.AluOpType.mult
COPY = mybir.ActivationFunctionType.Copy

P = 128
PACK = 4
S = E * C
BANDS = N // P
HALF = S // 2
RUN = 4

SCALAR_PLANES = (0, 1)
VECTOR_PLANES = (2, 3)


def tile_routed_moe_kernel(tc, xT, w, gate, offs, out):
    nc = tc.nc
    with ExitStack() as ctx:
        lists = ctx.enter_context(tc.tile_pool(name="lists", bufs=1))
        keep = ctx.enter_context(tc.tile_pool(name="keep", bufs=1))
        psum = ctx.enter_context(tc.psum_pool(name="psum", bufs=1))

        offsets = lists.tile([P, S // 16], U16, name="offsets")
        planes = [keep.tile([P, T], F32, name="plane%d" % t) for t in range(PACK)]
        w_raw = [keep.tile([P, PACK, N], F32, name="w_raw%d" % e, align_bytes=64) for e in range(E)]
        gate_sb = keep.tile([P, BANDS, S], F32, name="gate_sb")

        def load_plane(t):
            nc.sync.dma_start(planes[t][:], xT.rearrange("(p t) n -> p t n", t=PACK)[:, t, :])

        def load_weights(e):
            nc.sync.dma_start(w_raw[e][:], w[e].rearrange("(p j) n -> p j n", j=PACK))

        def load_gate(s0):
            nc.sync.dma_start(
                gate_sb[:, :, s0 : s0 + HALF], gate.rearrange("(b p) s -> p b s", p=P)[:, :, s0 : s0 + HALF]
            )

        load_plane(0)
        nc.sync.dma_start(offsets[:], offs)
        for t in range(1, PACK):
            load_plane(t)
        load_weights(0)
        load_weights(1)
        load_weights(2)
        load_gate(0)
        load_weights(3)
        load_gate(HALF)

        warm = keep.tile([P, 1], F32, name="warm")
        warm_out = keep.tile([P, 1], F32, name="warm_out")
        nc.vector.memset(warm[:], 0.0)
        nc.scalar.copy(warm_out[:], warm[:])

        windows = []
        for b in range(BANDS):
            window = keep.tile([P, T], F32, name="window%d" % b)
            nc.vector.memset(window[:], 0.0)
            windows.append(window)

        planes_bf = [keep.tile([P, T], BF16, name="plane_bf%d" % t) for t in SCALAR_PLANES]
        gathered = keep.tile([P, len(VECTOR_PLANES), S], F32, name="gathered")
        x_grouped = keep.tile([P, S, PACK], BF16, name="x_grouped", align_bytes=64)
        x_codes = [
            keep.tile([P, HALF], U32, name="x_codes0", align_bytes=64),
            keep.tile([P, HALF], U32, name="x_codes1", tag="w_raw0", align_bytes=64),
        ]
        x_scales = keep.tile([P, S], U8, name="x_scales", align_bytes=64)
        w_grouped = keep.tile([P, E * N, PACK], BF16, name="w_grouped", align_bytes=64)
        w0_grouped = keep.tile([P, N, PACK], BF16, name="w0_grouped", align_bytes=64)
        w1_band1 = keep.tile([P, P, PACK], BF16, name="w1_band1", tag="w0_grouped", align_bytes=64)

        def grouped_weights(e):
            return w0_grouped[:] if e == 0 else w_grouped[:, e * N : (e + 1) * N, :]

        w_codes = keep.tile([P, E * N], U32, name="w_codes", align_bytes=64)
        w_scales = keep.tile([P, E * N], U8, name="w_scales", align_bytes=64)
        acc = [[psum.tile([P, C], F32, name="acc%d_%d" % (e, b)) for b in range(BANDS)] for e in range(E)]
        y_sb = keep.tile([P, BANDS, S], F32, name="y_sb")

        def offsets_of(s0, n):
            return offsets[:, s0 // 16 : (s0 + n) // 16]

        def scalar_gather(t):
            nc.vector.tensor_copy(out=planes_bf[t][:], in_=planes[t][:])
            nc.scalar.activation(x_grouped[:, :, t], planes_bf[t][:].indirect(offsets[:]), COPY)

        def vector_gather(t, s0, n):
            nc.vector.tensor_copy(
                gathered[:, t - VECTOR_PLANES[0], s0 : s0 + n], planes[t][:].indirect(offsets_of(s0, n))
            )

        def round_vector_planes(s0, n):
            t0 = VECTOR_PLANES[0]
            nc.vector.tensor_copy(
                out=x_grouped[:, s0 : s0 + n, t0 : t0 + 2].rearrange("p (c i) t -> p c t i", i=RUN),
                in_=gathered[:, :, s0 : s0 + n].rearrange("p t (c i) -> p c t i", i=RUN),
            )

        def quantize_slots(s0, n):
            nc.vector.quantize_mx(
                out=x_codes[s0 // HALF][:].bitcast(FP8X4),
                scales=x_scales[:, s0 : s0 + n],
                in_=x_grouped[:, s0 : s0 + n, :].rearrange("p c t -> p (c t)"),
            )

        def group_weights(e):
            nc.scalar.copy(
                out=grouped_weights(e).rearrange("p (c i) j -> p c j i", i=RUN),
                in_=w_raw[e][:].rearrange("p j (c i) -> p c j i", i=RUN),
            )

        def group_w1_shared():
            nc.scalar.copy(
                out=w_grouped[:, N : N + P, :].rearrange("p (c i) j -> p c j i", i=RUN),
                in_=w_raw[1][:, :, :P].rearrange("p j (c i) -> p c j i", i=RUN),
            )
            nc.vector.tensor_copy(
                out=w1_band1[:].rearrange("p (c i) j -> p c j i", i=RUN),
                in_=w_raw[1][:, :, P:].rearrange("p j (c i) -> p c j i", i=RUN),
            )

        def quantize_weights(e):
            if e == 1:
                for b, grouped in enumerate((w_grouped[:, N : N + P, :], w1_band1[:])):
                    features = slice(N + b * P, N + (b + 1) * P)
                    nc.vector.quantize_mx(
                        out=w_codes[:, features].bitcast(FP8X4),
                        scales=w_scales[:, features],
                        in_=grouped.rearrange("p n j -> p (n j)"),
                    )
                return
            nc.vector.quantize_mx(
                out=w_codes[:, e * N : (e + 1) * N].bitcast(FP8X4),
                scales=w_scales[:, e * N : (e + 1) * N],
                in_=grouped_weights(e).rearrange("p n j -> p (n j)"),
            )

        def multiply(e):
            quantize_weights(e)
            slots = slice(e * C, (e + 1) * C)
            for b in range(BANDS):
                features = slice(e * N + b * P, e * N + (b + 1) * P)
                nc.tensor.matmul_mx(
                    out=acc[e][b][:],
                    lhsT=w_codes[:, features].bitcast(FP8X4),
                    lhsT_scale=w_scales[:, features],
                    rhs=x_codes[e * C // HALF][:, e * C % HALF : e * C % HALF + C].bitcast(FP8X4),
                    rhs_scale=x_scales[:, slots],
                    start=True,
                    stop=True,
                )
            for b in range(BANDS):
                nc.scalar.copy(out=y_sb[:, b, slots], in_=acc[e][b][:])

        def scatter(b, e):
            slots = slice(e * C, (e + 1) * C)
            nc.vector.tensor_tensor(
                windows[b][:].indirect(offsets_of(e * C, C)), y_sb[:, b, slots], gate_sb[:, b, slots], MULT
            )

        def store(b):
            nc.sync.dma_start(out[b * P : (b + 1) * P, :], windows[b][:])

        for t in SCALAR_PLANES:
            scalar_gather(t)
        vector_gather(2, 0, S)
        vector_gather(3, 0, HALF)
        round_vector_planes(0, HALF)
        vector_gather(3, HALF, HALF)
        group_weights(0)
        quantize_slots(0, HALF)
        multiply(0)
        round_vector_planes(HALF, HALF)
        quantize_slots(HALF, HALF)
        group_w1_shared()

        for e in range(1, E):
            scatter(0, e - 1)
            multiply(e)
            scatter(1, e - 1)
            if e + 1 < E:
                group_weights(e + 1)
        for b in range(BANDS):
            scatter(b, E - 1)
            store(b)
